import numpy as np
import ml_dtypes

BF16 = ml_dtypes.bfloat16


def bf(x):
    return np.asarray(x, np.float32).astype(BF16)


def f32(x):
    return np.asarray(x, np.float32)


def f64(x):
    return np.asarray(x).astype(np.float64)


def striped(idx):
    return np.concatenate([l.reshape(-1, 16).T for l in idx])


def rows(idx, k):
    return np.tile(np.repeat(idx, 16, axis=0), (k // (16 * 8), 1))


def look(tab, idx):
    return np.take_along_axis(f64(tab), rows(idx, len(tab)), axis=1)


K, S, V, N, M = 256, 2048, 1024, 1024, 256


def setup_inputs():
    return {"tab": f32(np.random.standard_normal((2, K, S))), "y": f32(1.0 * np.random.standard_normal((K, V))), "w": bf(np.random.standard_normal((K, M)) / np.sqrt(K)), "b": f32(0.5 * np.random.standard_normal((M, 1))), "offs": striped(np.stack([np.random.permutation(S)[:N] for _ in range(8)]))}


def reference(tab, y, w, b, offs):
    idx = np.stack([g.T.reshape(-1) for g in np.split(offs, 8)])
    x = np.maximum(look(tab[0], idx), f64(y)) * np.tanh(look(tab[1], idx))
    return np.maximum(f64(w).T @ x + f64(b), 0.0)

@@ -1,0 +1,85 @@
+import concourse.mybir as mybir
+
+F32, BF16, U16 = mybir.dt.float32, mybir.dt.bfloat16, mybir.dt.uint16
+MAX, MULT, ADD = mybir.AluOpType.max, mybir.AluOpType.mult, mybir.AluOpType.add
+TANH, RELU = mybir.ActivationFunctionType.Tanh, mybir.ActivationFunctionType.Relu
+
+P = 128
+ROWS = 256
+PLACES = 2048
+COLS = 1024
+OUTS = 256
+PIECE = 512
+
+FLOPS = 2 * ROWS * OUTS * COLS
+
+
+def tile_lookup_maxgate_relu_kernel(tc, tab, y, w, b, offs, out):
+    nc = tc.nc
+    row_blocks = ROWS // P
+    out_blocks = OUTS // P
+    pieces = COLS // PIECE
+
+    with (
+        tc.tile_pool(name="held", bufs=1) as held,
+        tc.psum_pool(name="psum", bufs=1) as psum,
+    ):
+        lists = held.tile([P, COLS // 16], U16, name="lists")
+        nc.sync.dma_start(lists[:], offs)
+
+        weights = held.tile([P, row_blocks, OUTS], BF16, name="weights")
+        nc.gpsimd.dma_start(weights[:], w.rearrange("(k p) m -> p k m", p=P))
+        biases = []
+        for m in range(out_blocks):
+            bias = held.tile([P, 1], F32, name=f"bias{m}")
+            nc.gpsimd.dma_start(bias[:], b[m * P : (m + 1) * P, :])
+            biases.append(bias)
+
+        floors, gates, streams = [], [], []
+        for k in range(row_blocks):
+            rows = slice(k * P, (k + 1) * P)
+            floor = held.tile([P, PLACES], F32, name=f"floor{k}")
+            nc.sync.dma_start(floor[:], tab[0, rows, :])
+            floors.append(floor)
+            stream = held.tile([P, COLS], F32, name=f"stream{k}")
+            nc.sync.dma_start(stream[:], y[rows, :])
+            streams.append(stream)
+            window = held.tile([P, PLACES], F32, name=f"window{k}")
+            nc.sync.dma_start(window[:], tab[1, rows, :])
+            gates.append(window)
+
+        products = [
+            [psum.tile([P, PIECE], F32, name=f"product{m}_{n}") for n in range(pieces)]
+            for m in range(out_blocks)
+        ]
+        for k in range(row_blocks):
+            for n in range(pieces):
+                columns = slice(n * PIECE, (n + 1) * PIECE)
+                entries = lists[:, n * PIECE // 16 : (n + 1) * PIECE // 16]
+
+                floored = held.tile([P, PIECE], F32, name=f"floored{k}_{n}")
+                nc.vector.tensor_tensor(floored[:], floors[k][:].indirect(entries), streams[k][:, columns], MAX)
+                gate = held.tile([P, PIECE], F32, name=f"gate{k}_{n}")
+                nc.scalar.activation(gate[:], gates[k][:].indirect(entries), TANH)
+
+                x = held.tile([P, PIECE], BF16, name=f"x{k}_{n}")
+                nc.vector.tensor_tensor(x[:], floored[:], gate[:], MULT)
+
+                for m in range(out_blocks):
+                    nc.tensor.matmul(
+                        products[m][n][:],
+                        weights[:, k, m * P : (m + 1) * P],
+                        x[:],
+                        start=(k == 0),
+                        stop=(k == row_blocks - 1),
+                    )
+
+        for n in range(pieces):
+            columns = slice(n * PIECE, (n + 1) * PIECE)
+            for m in range(out_blocks):
+                result = held.tile([P, PIECE], F32, name=f"result{m}_{n}")
+                if m % 2 == 0:
+                    nc.scalar.activation(result[:], products[m][n][:], RELU, bias=biases[m][:])
+                else:
+                    nc.vector.tensor_scalar(result[:], products[m][n][:], biases[m][:], 0.0, ADD, MAX)
+                nc.sync.dma_start(out[m * P : (m + 1) * P, columns], result[:])

@@ -10,6 +10,7 @@ PLACES = 2048
 COLS = 1024
 OUTS = 256
 PIECE = 512
+CHUNK = 256
 
 FLOPS = 2 * ROWS * OUTS * COLS
 
@@ -19,6 +20,7 @@ def tile_lookup_maxgate_relu_kernel(tc, tab, y, w, b, offs, out):
     row_blocks = ROWS // P
     out_blocks = OUTS // P
     pieces = COLS // PIECE
+    chunks = COLS // CHUNK
 
     with (
         tc.tile_pool(name="held", bufs=1) as held,
@@ -28,58 +30,61 @@ def tile_lookup_maxgate_relu_kernel(tc, tab, y, w, b, offs, out):
         nc.sync.dma_start(lists[:], offs)
 
         weights = held.tile([P, row_blocks, OUTS], BF16, name="weights")
-        nc.gpsimd.dma_start(weights[:], w.rearrange("(k p) m -> p k m", p=P))
-        biases = []
-        for m in range(out_blocks):
-            bias = held.tile([P, 1], F32, name=f"bias{m}")
-            nc.gpsimd.dma_start(bias[:], b[m * P : (m + 1) * P, :])
-            biases.append(bias)
+        nc.sync.dma_start(weights[:], w.rearrange("(k p) m -> p k m", p=P))
 
-        floors, gates, streams = [], [], []
+        floors, gates, streams = [], [], {}
         for k in range(row_blocks):
             rows = slice(k * P, (k + 1) * P)
             floor = held.tile([P, PLACES], F32, name=f"floor{k}")
             nc.sync.dma_start(floor[:], tab[0, rows, :])
             floors.append(floor)
-            stream = held.tile([P, COLS], F32, name=f"stream{k}")
-            nc.sync.dma_start(stream[:], y[rows, :])
-            streams.append(stream)
+            for n in range(pieces):
+                streams[k, n] = held.tile([P, PIECE], F32, name=f"stream{k}_{n}")
+            for n in range(pieces - 1):
+                nc.sync.dma_start(streams[k, n][:], y[rows, n * PIECE : (n + 1) * PIECE])
             window = held.tile([P, PLACES], F32, name=f"window{k}")
             nc.sync.dma_start(window[:], tab[1, rows, :])
             gates.append(window)
+            nc.sync.dma_start(streams[k, pieces - 1][:], y[rows, (pieces - 1) * PIECE :])
+
+        biases = []
+        for m in range(out_blocks):
+            bias = held.tile([P, 1], F32, name=f"bias{m}")
+            nc.sync.dma_start(bias[:], b[m * P : (m + 1) * P, :])
+            biases.append(bias)
 
         products = [
-            [psum.tile([P, PIECE], F32, name=f"product{m}_{n}") for n in range(pieces)]
+            [psum.tile([P, CHUNK], F32, name=f"product{m}_{c}") for c in range(chunks)]
             for m in range(out_blocks)
         ]
         for k in range(row_blocks):
             for n in range(pieces):
-                columns = slice(n * PIECE, (n + 1) * PIECE)
                 entries = lists[:, n * PIECE // 16 : (n + 1) * PIECE // 16]
 
                 floored = held.tile([P, PIECE], F32, name=f"floored{k}_{n}")
-                nc.vector.tensor_tensor(floored[:], floors[k][:].indirect(entries), streams[k][:, columns], MAX)
+                nc.vector.tensor_tensor(floored[:], floors[k][:].indirect(entries), streams[k, n][:], MAX)
                 gate = held.tile([P, PIECE], F32, name=f"gate{k}_{n}")
                 nc.scalar.activation(gate[:], gates[k][:].indirect(entries), TANH)
 
-                x = held.tile([P, PIECE], BF16, name=f"x{k}_{n}")
-                nc.vector.tensor_tensor(x[:], floored[:], gate[:], MULT)
+                for c in range(n * PIECE // CHUNK, (n + 1) * PIECE // CHUNK):
+                    inside = slice(c * CHUNK - n * PIECE, (c + 1) * CHUNK - n * PIECE)
+                    x = held.tile([P, CHUNK], BF16, name=f"x{k}_{c}")
+                    nc.vector.tensor_tensor(x[:], floored[:, inside], gate[:, inside], MULT)
+                    for m in range(out_blocks):
+                        nc.tensor.matmul(
+                            products[m][c][:],
+                            weights[:, k, m * P : (m + 1) * P],
+                            x[:],
+                            start=(k == 0),
+                            stop=(k == row_blocks - 1),
+                        )
 
-                for m in range(out_blocks):
-                    nc.tensor.matmul(
-                        products[m][n][:],
-                        weights[:, k, m * P : (m + 1) * P],
-                        x[:],
-                        start=(k == 0),
-                        stop=(k == row_blocks - 1),
-                    )
-
-        for n in range(pieces):
-            columns = slice(n * PIECE, (n + 1) * PIECE)
+        for c in range(chunks):
+            columns = slice(c * CHUNK, (c + 1) * CHUNK)
             for m in range(out_blocks):
-                result = held.tile([P, PIECE], F32, name=f"result{m}_{n}")
+                result = held.tile([P, CHUNK], F32, name=f"result{m}_{c}")
                 if m % 2 == 0:
-                    nc.scalar.activation(result[:], products[m][n][:], RELU, bias=biases[m][:])
+                    nc.scalar.activation(result[:], products[m][c][:], RELU, bias=biases[m][:])
                 else:
-                    nc.vector.tensor_scalar(result[:], products[m][n][:], biases[m][:], 0.0, ADD, MAX)
+                    nc.vector.tensor_scalar(result[:], products[m][c][:], biases[m][:], 0.0, ADD, MAX)
                 nc.sync.dma_start(out[m * P : (m + 1) * P, columns], result[:])

import concourse.mybir as mybir

F32, BF16, U16 = mybir.dt.float32, mybir.dt.bfloat16, mybir.dt.uint16
MAX, MULT, ADD = mybir.AluOpType.max, mybir.AluOpType.mult, mybir.AluOpType.add
TANH, RELU = mybir.ActivationFunctionType.Tanh, mybir.ActivationFunctionType.Relu

P = 128
ROWS = 256
PLACES = 2048
COLS = 1024
OUTS = 256
PIECE = 512
CHUNK = 256

FLOPS = 2 * ROWS * OUTS * COLS


def tile_lookup_maxgate_relu_kernel(tc, tab, y, w, b, offs, out):
    nc = tc.nc
    row_blocks = ROWS // P
    out_blocks = OUTS // P
    pieces = COLS // PIECE
    chunks = COLS // CHUNK

    with (
        tc.tile_pool(name="held", bufs=1) as held,
        tc.psum_pool(name="psum", bufs=1) as psum,
    ):
        lists = held.tile([P, COLS // 16], U16, name="lists")
        nc.sync.dma_start(lists[:], offs)

        weights = held.tile([P, row_blocks, OUTS], BF16, name="weights")
        nc.sync.dma_start(weights[:], w.rearrange("(k p) m -> p k m", p=P))

        floors, gates, streams = [], [], {}
        for k in range(row_blocks):
            rows = slice(k * P, (k + 1) * P)
            floor = held.tile([P, PLACES], F32, name=f"floor{k}")
            nc.sync.dma_start(floor[:], tab[0, rows, :])
            floors.append(floor)
            for n in range(pieces):
                streams[k, n] = held.tile([P, PIECE], F32, name=f"stream{k}_{n}")
            for n in range(pieces - 1):
                nc.sync.dma_start(streams[k, n][:], y[rows, n * PIECE : (n + 1) * PIECE])
            window = held.tile([P, PLACES], F32, name=f"window{k}")
            nc.sync.dma_start(window[:], tab[1, rows, :])
            gates.append(window)
            nc.sync.dma_start(streams[k, pieces - 1][:], y[rows, (pieces - 1) * PIECE :])

        biases = []
        for m in range(out_blocks):
            bias = held.tile([P, 1], F32, name=f"bias{m}")
            nc.sync.dma_start(bias[:], b[m * P : (m + 1) * P, :])
            biases.append(bias)

        products = [
            [psum.tile([P, CHUNK], F32, name=f"product{m}_{c}") for c in range(chunks)]
            for m in range(out_blocks)
        ]
        for k in range(row_blocks):
            for n in range(pieces):
                entries = lists[:, n * PIECE // 16 : (n + 1) * PIECE // 16]

                floored = held.tile([P, PIECE], F32, name=f"floored{k}_{n}")
                nc.vector.tensor_tensor(floored[:], floors[k][:].indirect(entries), streams[k, n][:], MAX)
                gate = held.tile([P, PIECE], F32, name=f"gate{k}_{n}")
                nc.scalar.activation(gate[:], gates[k][:].indirect(entries), TANH)

                for c in range(n * PIECE // CHUNK, (n + 1) * PIECE // CHUNK):
                    inside = slice(c * CHUNK - n * PIECE, (c + 1) * CHUNK - n * PIECE)
                    x = held.tile([P, CHUNK], BF16, name=f"x{k}_{c}")
                    nc.vector.tensor_tensor(x[:], floored[:, inside], gate[:, inside], MULT)
                    for m in range(out_blocks):
                        nc.tensor.matmul(
                            products[m][c][:],
                            weights[:, k, m * P : (m + 1) * P],
                            x[:],
                            start=(k == 0),
                            stop=(k == row_blocks - 1),
                        )

        for c in range(chunks):
            columns = slice(c * CHUNK, (c + 1) * CHUNK)
            for m in range(out_blocks):
                result = held.tile([P, CHUNK], F32, name=f"result{m}_{c}")
                if m % 2 == 0:
                    nc.scalar.activation(result[:], products[m][c][:], RELU, bias=biases[m][:])
                else:
                    nc.vector.tensor_scalar(result[:], products[m][c][:], biases[m][:], 0.0, ADD, MAX)
                nc.sync.dma_start(out[m * P : (m + 1) * P, columns], result[:])
